import numpy as np
import ml_dtypes


def mxq(x, axis, fmt="e4m3"):
    dtype, down = {"e4m3": (ml_dtypes.float8_e4m3fn, 7), "e5m2": (ml_dtypes.float8_e5m2, 14)}[fmt]
    v = np.moveaxis(np.asarray(x, np.float32).astype(ml_dtypes.bfloat16).astype(np.float64), axis, -1)
    blocks = v.reshape(v.shape[:-1] + (-1, 32))
    amax = np.abs(blocks).max(-1, keepdims=True)
    byte = np.maximum(np.where(amax > 0, np.frexp(amax)[1] - 1 + 127, 0) - down, 1)
    scale = np.exp2(byte - 127.0)
    codes = (blocks / scale).astype(np.float32).astype(dtype).astype(np.float64)
    return np.moveaxis((codes * scale).reshape(v.shape), -1, axis)


WIDE = False


def mx_kscale(k):
    if not WIDE:
        return np.ones(k)
    levels = np.array([10, -10, 5, -5, 0])
    if k % 512:
        return np.exp2(np.random.permutation(np.resize(levels, k // 32))).repeat(32)
    a = np.empty((k // 512, 16))
    for p in range(k // 512):
        a[p, :8] = np.random.permutation(np.resize(levels, 8))
        for g in range(8):
            far = levels[np.abs(levels - a[p, g]) >= 10]
            a[p, g + 8] = far[np.random.randint(len(far))]
    return np.exp2(a.ravel()).repeat(32)


def f64(x):
    return np.asarray(x).astype(np.float64)


def striped(idx):
    return np.tile(idx.reshape(-1, 16).T, (8, 1)).astype(np.uint16)


def unstriped(offs):
    return offs[:16].T.reshape(-1).astype(np.int64)


def pack_weight(w):
    k, n = w.shape
    w = f64(np.asarray(w, np.float32).astype(ml_dtypes.bfloat16)).reshape(k // 32, 32, n)
    amax = np.abs(w).max(1)
    byte = np.clip(np.where(amax > 0, np.frexp(amax)[1] - 1 + 127 - 7, 1), 1, 254)
    scaled = (w * np.exp2(127.0 - byte)[:, None, :]).reshape(k, n).astype(np.float32)
    words = np.ascontiguousarray(scaled.reshape(k // 512, 128, 4, n).transpose(0, 1, 3, 2)).astype(ml_dtypes.float8_e4m3fn).view(np.uint8)
    return words, np.ascontiguousarray(byte.astype(np.uint8).reshape(k // 512, 16, n))


def unpack_weight(words, scales):
    g, p, n, _ = words.shape
    vals = np.ascontiguousarray(words).view(ml_dtypes.float8_e4m3fn).astype(np.float64) * np.repeat(np.exp2(scales.astype(np.float64) - 127.0), 8, axis=1)[..., None]
    return vals.transpose(0, 1, 3, 2).reshape(g * 512, n)


def relu(v):
    return np.maximum(v, 0.0)


K, T, S, V = 512, 2048, 512, 512
P = 2 ** 7


def setup_inputs():
    n = np.random.standard_normal
    s = mx_kscale(K)[:, None]
    packed_xT = pack_weight(n((K, T)) * s)
    return {
        "x_words": packed_xT[0],
        "x_scales": packed_xT[1],
        "hT": (n((K, V)) / np.sqrt(K) / s).astype(np.float32),
        "proj": (0.6 * n((V, S))).astype(np.float32),
        "dres": (np.random.uniform(0.4, 2.0, (V, S))).astype(np.float32),
        "qual": (np.tile(np.random.uniform(0.5, 1.5, T), (P, 1))).astype(np.float32),
        "inv": (np.random.uniform(0.3, 0.7, (V, 1))).astype(np.float32),
        "offs": striped(np.random.permutation(T)[:S]),
    }


def reference(x_words, x_scales, hT, proj, dres, qual, inv, offs):
    hTq = mxq(f64(hT), 0, "e4m3")
    xq = unpack_weight(x_words, x_scales)[:, unstriped(offs)]
    y = hTq.T @ xq
    ee = f64(inv) * ((f64(qual)[:1][:, unstriped(offs)]) * y - f64(proj))
    dnew = relu(f64(dres) - ((ee) ** 2)) + 0.02
    top = dnew.max(axis=1, keepdims=True)
    return (dnew / top) * (f64(qual)[:1][:, unstriped(offs)]) - (0.2 * np.abs(ee))

@@ -1,0 +1,215 @@
+from contextlib import ExitStack
+
+import concourse.mybir as mybir
+
+K, T, S, V = 512, 2048, 512, 512
+FLOPS = 2 * K * S * V
+
+F32 = mybir.dt.float32
+BF16 = mybir.dt.bfloat16
+I32 = mybir.dt.int32
+U32 = mybir.dt.uint32
+U16 = mybir.dt.uint16
+U8 = mybir.dt.uint8
+FP8X4 = mybir.dt.float8_e4m3fn_x4
+ALU = mybir.AluOpType
+ACT = mybir.ActivationFunctionType
+
+P = 128
+PACK = 4
+TILES = V // P
+BLOCKS = S // P
+HALF = S // 2
+FLOOR = 0.02
+POOL_TILES = (0, 1, 2)
+
+
+def tile_picked_ydppg_rel_p_kernel(tc, x_words, x_scales, hT, proj, dres, qual, inv, offs, out):
+    nc = tc.nc
+    with ExitStack() as ctx:
+        keep = ctx.enter_context(tc.tile_pool(name="keep", bufs=1))
+        psum = ctx.enter_context(tc.psum_pool(name="psum", bufs=1))
+
+        offsets = keep.tile([P, S // 16], U16, name="offsets")
+        nc.sync.dma_start(offsets[:], offs)
+
+        scale_win = keep.tile([P, T], U8, name="scale_win")
+        nc.vector.memset(scale_win[:].bitcast(I32), 0)
+        for quad in range(4):
+            nc.scalar.dma_start(
+                scale_win[32 * quad : 32 * quad + 4, :].bitcast(I32),
+                x_scales[0, 4 * quad : 4 * quad + 4, :].bitcast(I32),
+            )
+
+        word_win = keep.tile([P, T], U32, name="word_win")
+        nc.sync.dma_start(word_win[:].bitcast(I32), x_words[0].rearrange("p n t -> p (n t)").bitcast(I32))
+
+        qual_win = keep.tile([P, T], F32, name="qual_win", tag="qual", align_bytes=64)
+        nc.vector.memset(qual_win[:], 0.0)
+        nc.scalar.dma_start(qual_win[0:1, :], qual[0:1, :])
+
+        zeros = keep.tile([P, P], F32, name="zeros", tag="stage")
+        nc.vector.memset(zeros[:], 0.0)
+        ident = keep.tile([P, P], F32, name="ident")
+        nc.gpsimd.affine_select(
+            out=ident[:], in_=zeros[:], compare_op=ALU.not_equal, fill=1.0, base=0, pattern=[[-1, P]], channel_multiplier=1
+        )
+
+        stage = keep.tile([P, 3 * TILES * S + TILES], F32, name="stage", tag="stage")
+        proj_sb = [stage[:, i * S : (i + 1) * S] for i in range(TILES)]
+        dres_sb = [stage[:, (TILES + i) * S : (TILES + i + 1) * S] for i in range(TILES)]
+        h_rows = hT.rearrange("(p j) w -> p j w", j=PACK)
+        h_sb = stage[:, 2 * TILES * S : 3 * TILES * S]
+        h_one = [h_sb[:, i * S : (i + 1) * S].rearrange("p (j w) -> p j w", j=PACK) for i in range(2)]
+        h_second = h_sb[:, 2 * S :].rearrange("p (j w) -> p j w", j=PACK)
+        h_raw = h_one + [h_second[:, :, c * P : (c + 1) * P] for c in range(2)]
+
+        def load(sb, src, i):
+            nc.sync.dma_start(sb[i], src[i * P : (i + 1) * P, :])
+
+        for i in range(2):
+            nc.sync.dma_start(h_one[i], h_rows[:, :, i * P : (i + 1) * P])
+        load(proj_sb, proj, 0)
+        load(proj_sb, proj, 1)
+        nc.sync.dma_start(h_second, h_rows[:, :, 2 * P : V])
+        load(dres_sb, dres, 0)
+        load(dres_sb, dres, 1)
+        for i in range(2, TILES):
+            load(proj_sb, proj, i)
+            load(dres_sb, dres, i)
+
+        inv_sb = stage[:, 3 * TILES * S :]
+        with nc.allow_non_contiguous_dma(reason="one value a partition"):
+            nc.scalar.dma_start(inv_sb, inv.rearrange("(c p) o -> p (c o)", p=P))
+        inv_fifth = keep.tile([P, TILES], F32, name="inv_fifth")
+        nc.gpsimd.tensor_scalar(inv_fifth[:], inv_sb, 0.2, 0.0, ALU.mult, ALU.add)
+
+        h_codes, h_scales = [], []
+
+        def cast(i):
+            grouped = keep.tile([P, P, PACK], BF16, name="h_bf%d" % i, align_bytes=64)
+            nc.scalar.activation(
+                grouped[:].rearrange("p (c e) j -> p c j e", e=4),
+                h_raw[i].rearrange("p j (c e) -> p c j e", e=4),
+                ACT.Copy,
+            )
+            return grouped
+
+        def quantise(i, grouped):
+            h_codes.append(keep.tile([P, P], U32, name="h_codes%d" % i, align_bytes=64))
+            h_scales.append(keep.tile([P, P], U8, name="h_scales%d" % i, align_bytes=64))
+            nc.vector.quantize_mx(
+                out=h_codes[i][:].bitcast(FP8X4),
+                scales=h_scales[i][:],
+                in_=grouped[:].rearrange("p w j -> p (w j)"),
+            )
+
+        grouped0 = cast(0)
+        grouped1 = cast(1)
+        x_bytes = keep.tile([P, S], U8, name="x_bytes", align_bytes=64)
+        nc.vector.tensor_copy(x_bytes[:], scale_win[:].indirect(offsets[:]))
+        q_row = keep.tile([P, S], F32, name="q_row")
+        nc.vector.tensor_copy(q_row[:], qual_win[:].indirect(offsets[:]))
+        x_all = keep.tile([P, S], U32, name="x_all", tag="qual", align_bytes=64)
+        x_codes = [x_all[:, h * HALF : (h + 1) * HALF] for h in range(2)]
+        for h in range(2):
+            nc.vector.tensor_copy(x_codes[h], word_win[:].indirect(offsets[:, h * 16 : (h + 1) * 16]))
+        quantise(0, grouped0)
+        quantise(1, grouped1)
+
+        q_turned = psum.tile([P, BLOCKS, P], F32, name="q_turned", tag="qy", bufs=3)
+        for b in range(BLOCKS):
+            nc.tensor.transpose(q_turned[:, b, :], q_row[:, b * P : (b + 1) * P], ident[:])
+        q_col = keep.tile([P, BLOCKS], F32, name="q_col")
+        nc.scalar.copy(q_col[:], q_turned[:, :, 0])
+        q_wide = psum.tile([P, S], F32, name="q_wide")
+        for b in range(BLOCKS):
+            nc.tensor.transpose(q_wide[:, b * P : (b + 1) * P], q_col[:, b : b + 1].to_broadcast([P, P]), ident[:])
+
+        diff, square, fifth, rest, dnew, top, rtop, gain = {}, {}, {}, {}, {}, {}, {}, {}
+
+        def product(i):
+            scaled = keep.tile([P, BLOCKS, P], F32, name="scaled%d" % i)
+            qy = psum.tile([P, S], F32, name="qy%d" % i, tag="qy", bufs=3)
+            for h in range(2):
+                y_t = psum.tile([P, 2, P], F32, name="y_t%d_%d" % (i, h), tag="y_t", bufs=4)
+                for c in range(2):
+                    b = 2 * h + c
+                    nc.tensor.matmul_mx(
+                        out=y_t[:, c, :],
+                        lhsT=x_codes[h][:, c * P : (c + 1) * P].bitcast(FP8X4),
+                        lhsT_scale=x_bytes[:, b * P : (b + 1) * P],
+                        rhs=h_codes[i][:].bitcast(FP8X4),
+                        rhs_scale=h_scales[i][:],
+                        start=True,
+                        stop=True,
+                    )
+                for c in range(2):
+                    b = 2 * h + c
+                    nc.scalar.activation(scaled[:, b, :], y_t[:, c, :], ACT.Copy, scale=q_col[:, b : b + 1])
+            for b in range(BLOCKS):
+                nc.tensor.transpose(qy[:, b * P : (b + 1) * P], scaled[:, b, :], ident[:])
+            return qy
+
+        def difference(i, qy):
+            diff[i] = keep.tile([P, S], F32, name="diff%d" % i)
+            nc.vector.tensor_tensor(diff[i][:], qy[:], proj_sb[i], ALU.subtract)
+            square[i] = keep.tile([P, S], F32, name="square%d" % i)
+            nc.scalar.activation(square[i][:], diff[i][:], ACT.Square, scale=inv_sb[:, i : i + 1])
+
+        def size(i):
+            fifth[i] = keep.tile([P, S], F32, name="fifth%d" % i)
+            nc.scalar.activation(fifth[i][:], diff[i][:], ACT.Abs, scale=inv_fifth[:, i : i + 1])
+
+        def remainder(i):
+            rest[i] = keep.tile([P, S], F32, name="rest%d" % i)
+            nc.vector.scalar_tensor_tensor(rest[i][:], dres_sb[i], FLOOR, square[i][:], ALU.add, ALU.subtract)
+
+        def best(i):
+            dnew[i] = keep.tile([P, S], F32, name="dnew%d" % i)
+            top[i] = keep.tile([P, 1], F32, name="top%d" % i)
+            nc.vector.tensor_scalar(dnew[i][:], rest[i][:], FLOOR, None, ALU.max, ALU.max, accum_out=top[i][:])
+
+        def invert(i):
+            rtop[i] = keep.tile([P, 1], F32, name="rtop%d" % i)
+            nc.vector.reciprocal(rtop[i][:], top[i][:])
+
+        def finish(i):
+            gain[i] = keep.tile([P, S], F32, name="gain%d" % i)
+            nc.vector.scalar_tensor_tensor(gain[i][:], dnew[i][:], rtop[i][:], q_wide[:], ALU.mult, ALU.mult)
+            result = keep.tile([P, S], F32, name="result%d" % i)
+            engine = nc.gpsimd if i in POOL_TILES else nc.vector
+            engine.tensor_tensor(result[:], gain[i][:], fifth[i][:], ALU.subtract)
+            nc.sync.dma_start(out[i * P : (i + 1) * P, :], result[:])
+
+        qy0 = product(0)
+        qy1 = product(1)
+        grouped2 = cast(2)
+        difference(0, qy0)
+        difference(1, qy1)
+        quantise(2, grouped2)
+        qy2 = product(2)
+        remainder(0)
+        best(0)
+        quantise(3, cast(3))
+        remainder(1)
+        difference(2, qy2)
+        qy3 = product(3)
+        size(0)
+        invert(0)
+        finish(0)
+        best(1)
+        difference(3, qy3)
+        size(1)
+        remainder(2)
+        invert(1)
+        remainder(3)
+        finish(1)
+        size(2)
+        size(3)
+        best(2)
+        best(3)
+        invert(2)
+        invert(3)
+        finish(2)
+        finish(3)

@@ -21,7 +21,9 @@ TILES = V // P
 BLOCKS = S // P
 HALF = S // 2
 FLOOR = 0.02
-POOL_TILES = (0, 1, 2)
+PE_TILES = ()
+TURN_TILES = ()
+DIRECT_TILES = (0, 1, 2, 3)
 
 
 def tile_picked_ydppg_rel_p_kernel(tc, x_words, x_scales, hT, proj, dres, qual, inv, offs, out):
@@ -33,20 +35,21 @@ def tile_picked_ydppg_rel_p_kernel(tc, x_words, x_scales, hT, proj, dres, qual, 
         offsets = keep.tile([P, S // 16], U16, name="offsets")
         nc.sync.dma_start(offsets[:], offs)
 
-        scale_win = keep.tile([P, T], U8, name="scale_win")
+        q_rows = keep.tile([P, T // P], F32, name="q_rows")
+        nc.sync.dma_start(q_rows[:], qual[0:1, :].rearrange("o (p c) -> (o p) c", p=P))
+        h_rows = hT.rearrange("(p j) w -> p j w", j=PACK)
+        h_first = keep.tile([P, PACK, P], F32, name="h_first")
+        nc.sync.dma_start(h_first[:], h_rows[:, :, 0:P])
+        word_win = keep.tile([P, T], U32, name="word_win")
+        nc.sync.dma_start(word_win[:].bitcast(I32), x_words[0].rearrange("p n t -> p (n t)").bitcast(I32))
+
+        scale_win = keep.tile([P, T], U8, name="scale_win", tag="scales", align_bytes=64)
         nc.vector.memset(scale_win[:].bitcast(I32), 0)
         for quad in range(4):
             nc.scalar.dma_start(
                 scale_win[32 * quad : 32 * quad + 4, :].bitcast(I32),
                 x_scales[0, 4 * quad : 4 * quad + 4, :].bitcast(I32),
             )
-
-        word_win = keep.tile([P, T], U32, name="word_win")
-        nc.sync.dma_start(word_win[:].bitcast(I32), x_words[0].rearrange("p n t -> p (n t)").bitcast(I32))
-
-        qual_win = keep.tile([P, T], F32, name="qual_win", tag="qual", align_bytes=64)
-        nc.vector.memset(qual_win[:], 0.0)
-        nc.scalar.dma_start(qual_win[0:1, :], qual[0:1, :])
 
         zeros = keep.tile([P, P], F32, name="zeros", tag="stage")
         nc.vector.memset(zeros[:], 0.0)
@@ -55,34 +58,29 @@ def tile_picked_ydppg_rel_p_kernel(tc, x_words, x_scales, hT, proj, dres, qual, 
             out=ident[:], in_=zeros[:], compare_op=ALU.not_equal, fill=1.0, base=0, pattern=[[-1, P]], channel_multiplier=1
         )
 
-        stage = keep.tile([P, 3 * TILES * S + TILES], F32, name="stage", tag="stage")
+        stage = keep.tile([P, (3 * TILES - 1) * S + P], F32, name="stage", tag="stage")
         proj_sb = [stage[:, i * S : (i + 1) * S] for i in range(TILES)]
         dres_sb = [stage[:, (TILES + i) * S : (TILES + i + 1) * S] for i in range(TILES)]
-        h_rows = hT.rearrange("(p j) w -> p j w", j=PACK)
-        h_sb = stage[:, 2 * TILES * S : 3 * TILES * S]
-        h_one = [h_sb[:, i * S : (i + 1) * S].rearrange("p (j w) -> p j w", j=PACK) for i in range(2)]
-        h_second = h_sb[:, 2 * S :].rearrange("p (j w) -> p j w", j=PACK)
-        h_raw = h_one + [h_second[:, :, c * P : (c + 1) * P] for c in range(2)]
+        h_second = stage[:, 2 * TILES * S : (2 * TILES + 1) * S].rearrange("p (j w) -> p j w", j=PACK)
+        h_last = stage[:, (2 * TILES + 1) * S : (3 * TILES - 1) * S].rearrange("p (j w) -> p j w", j=PACK)
+        h_raw = [h_first[:], h_second, h_last[:, :, 0:P], h_last[:, :, P : 2 * P]]
+        inv_rows = stage[:, (3 * TILES - 1) * S :]
+        nc.vector.memset(inv_rows, 0.0)
+        nc.sync.dma_start(inv_rows[0:TILES, :], inv.rearrange("(c p) o -> c (p o)", p=P))
 
         def load(sb, src, i):
             nc.sync.dma_start(sb[i], src[i * P : (i + 1) * P, :])
 
-        for i in range(2):
-            nc.sync.dma_start(h_one[i], h_rows[:, :, i * P : (i + 1) * P])
+        nc.sync.dma_start(h_second, h_rows[:, :, P : 2 * P])
         load(proj_sb, proj, 0)
         load(proj_sb, proj, 1)
-        nc.sync.dma_start(h_second, h_rows[:, :, 2 * P : V])
+        nc.sync.dma_start(h_last, h_rows[:, :, 2 * P : V])
         load(dres_sb, dres, 0)
         load(dres_sb, dres, 1)
-        for i in range(2, TILES):
-            load(proj_sb, proj, i)
-            load(dres_sb, dres, i)
-
-        inv_sb = stage[:, 3 * TILES * S :]
-        with nc.allow_non_contiguous_dma(reason="one value a partition"):
-            nc.scalar.dma_start(inv_sb, inv.rearrange("(c p) o -> p (c o)", p=P))
-        inv_fifth = keep.tile([P, TILES], F32, name="inv_fifth")
-        nc.gpsimd.tensor_scalar(inv_fifth[:], inv_sb, 0.2, 0.0, ALU.mult, ALU.add)
+        load(proj_sb, proj, 2)
+        load(dres_sb, dres, 2)
+        load(proj_sb, proj, 3)
+        load(dres_sb, dres, 3)
 
         h_codes, h_scales = [], []
 
@@ -105,55 +103,93 @@ def tile_picked_ydppg_rel_p_kernel(tc, x_words, x_scales, hT, proj, dres, qual, 
             )
 
         grouped0 = cast(0)
-        grouped1 = cast(1)
+        qual_win = keep.tile([P, T], F32, name="qual_win")
+        for g in range(4):
+            spread = psum.tile([P, 4, P], F32, name="spread%d" % g, tag="turned", bufs=3)
+            for c in range(4):
+                col = 4 * g + c
+                nc.tensor.transpose(spread[:, c, :], q_rows[:, col : col + 1].to_broadcast([P, P]), ident[:])
+            nc.scalar.copy(
+                qual_win[:].rearrange("p (m c) -> p m c", c=T // P)[:, :, 4 * g : 4 * g + 4],
+                spread[:].rearrange("p c m -> p m c"),
+            )
+
         x_bytes = keep.tile([P, S], U8, name="x_bytes", align_bytes=64)
         nc.vector.tensor_copy(x_bytes[:], scale_win[:].indirect(offsets[:]))
-        q_row = keep.tile([P, S], F32, name="q_row")
-        nc.vector.tensor_copy(q_row[:], qual_win[:].indirect(offsets[:]))
-        x_all = keep.tile([P, S], U32, name="x_all", tag="qual", align_bytes=64)
-        x_codes = [x_all[:, h * HALF : (h + 1) * HALF] for h in range(2)]
-        for h in range(2):
-            nc.vector.tensor_copy(x_codes[h], word_win[:].indirect(offsets[:, h * 16 : (h + 1) * 16]))
         quantise(0, grouped0)
-        quantise(1, grouped1)
+        x_all = keep.tile([P, S], U32, name="x_all", tag="scales", align_bytes=64)
+        nc.vector.tensor_copy(x_all[:], word_win[:].indirect(offsets[:]))
+        q_sb = keep.tile([P, S], F32, name="q_sb")
+        nc.vector.tensor_copy(q_sb[:], qual_win[:].indirect(offsets[:]))
 
-        q_turned = psum.tile([P, BLOCKS, P], F32, name="q_turned", tag="qy", bufs=3)
-        for b in range(BLOCKS):
-            nc.tensor.transpose(q_turned[:, b, :], q_row[:, b * P : (b + 1) * P], ident[:])
-        q_col = keep.tile([P, BLOCKS], F32, name="q_col")
-        nc.scalar.copy(q_col[:], q_turned[:, :, 0])
-        q_wide = psum.tile([P, S], F32, name="q_wide")
-        for b in range(BLOCKS):
-            nc.tensor.transpose(q_wide[:, b * P : (b + 1) * P], q_col[:, b : b + 1].to_broadcast([P, P]), ident[:])
+        inv_turned = psum.tile([P, P], F32, name="inv_turned", tag="turned", bufs=3)
+        nc.tensor.transpose(inv_turned[:], inv_rows, ident[:])
+        inv_sb = keep.tile([P, TILES], F32, name="inv_sb")
+        nc.scalar.copy(inv_sb[:], inv_turned[:, 0:TILES])
+        inv_fifth = keep.tile([P, TILES], F32, name="inv_fifth")
+        nc.scalar.activation(inv_fifth[:], inv_turned[:, 0:TILES], ACT.Copy, scale=0.2)
+        quantise(1, cast(1))
 
-        diff, square, fifth, rest, dnew, top, rtop, gain = {}, {}, {}, {}, {}, {}, {}, {}
+        q_col = None
+        minus, diff, square, fifth, rest, dnew, top, rtop, gain = {}, {}, {}, {}, {}, {}, {}, {}, {}
+
+        def turned_proj(i):
+            turned = psum.tile([P, S], F32, name="turned%d" % i, tag="turned", bufs=3)
+            for b in range(BLOCKS):
+                nc.tensor.transpose(turned[:, b * P : (b + 1) * P], proj_sb[i][:, b * P : (b + 1) * P], ident[:])
+            minus[i] = keep.tile([P, S], F32, name="minus%d" % i)
+            nc.scalar.activation(minus[i][:], turned[:], ACT.Copy, scale=-1.0)
 
         def product(i):
-            scaled = keep.tile([P, BLOCKS, P], F32, name="scaled%d" % i)
             qy = psum.tile([P, S], F32, name="qy%d" % i, tag="qy", bufs=3)
-            for h in range(2):
-                y_t = psum.tile([P, 2, P], F32, name="y_t%d_%d" % (i, h), tag="y_t", bufs=4)
-                for c in range(2):
-                    b = 2 * h + c
+            if i in DIRECT_TILES:
+                nc.tensor.matmul_mx(
+                    out=qy[:],
+                    lhsT=h_codes[i][:].bitcast(FP8X4),
+                    lhsT_scale=h_scales[i][:],
+                    rhs=x_all[:].bitcast(FP8X4),
+                    rhs_scale=x_bytes[:],
+                    start=True,
+                    stop=True,
+                )
+                weighted = keep.tile([P, S], F32, name="weighted%d" % i)
+                nc.vector.tensor_tensor(weighted[:], qy[:], q_sb[:], ALU.mult)
+                return weighted
+            scaled = keep.tile([P, BLOCKS, P], F32, name="scaled%d" % i)
+            width = BLOCKS
+            for first in range(0, BLOCKS, width):
+                y_t = psum.tile([P, width, P], F32, name="y_t%d_%d" % (i, first), tag="y_t", bufs=2)
+                for c in range(width):
+                    b = first + c
                     nc.tensor.matmul_mx(
                         out=y_t[:, c, :],
-                        lhsT=x_codes[h][:, c * P : (c + 1) * P].bitcast(FP8X4),
+                        lhsT=x_all[:, b * P : (b + 1) * P].bitcast(FP8X4),
                         lhsT_scale=x_bytes[:, b * P : (b + 1) * P],
                         rhs=h_codes[i][:].bitcast(FP8X4),
                         rhs_scale=h_scales[i][:],
                         start=True,
                         stop=True,
                     )
-                for c in range(2):
-                    b = 2 * h + c
+                for c in range(width):
+                    b = first + c
                     nc.scalar.activation(scaled[:, b, :], y_t[:, c, :], ACT.Copy, scale=q_col[:, b : b + 1])
             for b in range(BLOCKS):
-                nc.tensor.transpose(qy[:, b * P : (b + 1) * P], scaled[:, b, :], ident[:])
+                cols = slice(b * P, (b + 1) * P)
+                if i in PE_TILES:
+                    nc.tensor.matmul(qy[:, cols], minus[i][:, cols], ident[:], start=True, stop=False, is_transpose=True)
+                    nc.tensor.matmul(qy[:, cols], scaled[:, b, :], ident[:], start=False, stop=True, is_transpose=True)
+                else:
+                    nc.tensor.transpose(qy[:, cols], scaled[:, b, :], ident[:])
             return qy
 
         def difference(i, qy):
-            diff[i] = keep.tile([P, S], F32, name="diff%d" % i)
-            nc.vector.tensor_tensor(diff[i][:], qy[:], proj_sb[i], ALU.subtract)
+            if i in PE_TILES:
+                diff[i] = qy
+            else:
+                diff[i] = keep.tile([P, S], F32, name="diff%d" % i)
+                nc.vector.tensor_tensor(diff[i][:], qy[:], proj_sb[i], ALU.subtract)
+
+        def squared(i):
             square[i] = keep.tile([P, S], F32, name="square%d" % i)
             nc.scalar.activation(square[i][:], diff[i][:], ACT.Square, scale=inv_sb[:, i : i + 1])
 
@@ -174,42 +210,74 @@ def tile_picked_ydppg_rel_p_kernel(tc, x_words, x_scales, hT, proj, dres, qual, 
             rtop[i] = keep.tile([P, 1], F32, name="rtop%d" % i)
             nc.vector.reciprocal(rtop[i][:], top[i][:])
 
-        def finish(i):
+        def weigh(i, cols):
+            if i not in TURN_TILES:
+                nc.vector.scalar_tensor_tensor(gain[i][:, cols], dnew[i][:, cols], rtop[i][:], q_sb[:, cols], ALU.mult, ALU.mult)
+                return
+            dnew_t = psum.tile([P, BLOCKS, P], F32, name="dnew_t%d" % i, tag="turned", bufs=3)
+            for b in range(BLOCKS):
+                nc.tensor.transpose(dnew_t[:, b, :], dnew[i][:, b * P : (b + 1) * P], ident[:])
+            for b in range(BLOCKS):
+                nc.scalar.activation(gain[i][:, b * P : (b + 1) * P], dnew_t[:, b, :], ACT.Copy, scale=q_col[:, b : b + 1])
+            back[i] = psum.tile([P, S], F32, name="back%d" % i, tag="qy", bufs=3)
+            for b in range(BLOCKS):
+                nc.tensor.transpose(back[i][:, b * P : (b + 1) * P], gain[i][:, b * P : (b + 1) * P], ident[:])
+
+        def finish(i, cols):
+            if i in TURN_TILES:
+                nc.vector.scalar_tensor_tensor(
+                    result[i][:, cols], back[i][:, cols], rtop[i][:], fifth[i][:, cols], ALU.mult, ALU.subtract
+                )
+            else:
+                nc.vector.tensor_tensor(result[i][:, cols], gain[i][:, cols], fifth[i][:, cols], ALU.subtract)
+            nc.sync.dma_start(out[i * P : (i + 1) * P, cols], result[i][:, cols])
+
+        back = {}
+        result = {}
+        for i in range(TILES):
             gain[i] = keep.tile([P, S], F32, name="gain%d" % i)
-            nc.vector.scalar_tensor_tensor(gain[i][:], dnew[i][:], rtop[i][:], q_wide[:], ALU.mult, ALU.mult)
-            result = keep.tile([P, S], F32, name="result%d" % i)
-            engine = nc.gpsimd if i in POOL_TILES else nc.vector
-            engine.tensor_tensor(result[:], gain[i][:], fifth[i][:], ALU.subtract)
-            nc.sync.dma_start(out[i * P : (i + 1) * P, :], result[:])
+            result[i] = keep.tile([P, S], F32, name="result%d" % i)
+        whole, left, right = slice(0, S), slice(0, HALF), slice(HALF, S)
 
         qy0 = product(0)
+        difference(0, qy0)
+        squared(0)
         qy1 = product(1)
         grouped2 = cast(2)
-        difference(0, qy0)
         difference(1, qy1)
+        squared(1)
         quantise(2, grouped2)
-        qy2 = product(2)
+        grouped3 = cast(3)
         remainder(0)
-        best(0)
-        quantise(3, cast(3))
-        remainder(1)
-        difference(2, qy2)
-        qy3 = product(3)
+        quantise(3, grouped3)
         size(0)
+        best(0)
+        qy2 = product(2)
         invert(0)
-        finish(0)
-        best(1)
-        difference(3, qy3)
+        remainder(1)
+        weigh(0, whole)
+        difference(2, qy2)
+        squared(2)
+        finish(0, whole)
         size(1)
-        remainder(2)
+        best(1)
+        qy3 = product(3)
         invert(1)
-        remainder(3)
-        finish(1)
+        difference(3, qy3)
+        squared(3)
+        weigh(1, whole)
+        remainder(2)
+        finish(1, whole)
         size(2)
         size(3)
         best(2)
-        best(3)
+        remainder(3)
         invert(2)
+        best(3)
+        weigh(2, whole)
         invert(3)
-        finish(2)
-        finish(3)
+        finish(2, whole)
+        weigh(3, left)
+        weigh(3, right)
+        finish(3, left)
+        finish(3, right)

@@ -22,14 +22,15 @@ BLOCKS = S // P
 HALF = S // 2
 FLOOR = 0.02
 PE_TILES = ()
-TURN_TILES = ()
-DIRECT_TILES = (0, 1, 2, 3)
+TURN_TILES = (0, 1, 2)
+DIRECT_TILES = (0, 1, 2)
 
 
 def tile_picked_ydppg_rel_p_kernel(tc, x_words, x_scales, hT, proj, dres, qual, inv, offs, out):
     nc = tc.nc
     with ExitStack() as ctx:
         keep = ctx.enter_context(tc.tile_pool(name="keep", bufs=1))
+        late = ctx.enter_context(tc.tile_pool(name="late", bufs=1))
         psum = ctx.enter_context(tc.psum_pool(name="psum", bufs=1))
 
         offsets = keep.tile([P, S // 16], U16, name="offsets")
@@ -40,8 +41,6 @@ def tile_picked_ydppg_rel_p_kernel(tc, x_words, x_scales, hT, proj, dres, qual, 
         h_rows = hT.rearrange("(p j) w -> p j w", j=PACK)
         h_first = keep.tile([P, PACK, P], F32, name="h_first")
         nc.sync.dma_start(h_first[:], h_rows[:, :, 0:P])
-        word_win = keep.tile([P, T], U32, name="word_win")
-        nc.sync.dma_start(word_win[:].bitcast(I32), x_words[0].rearrange("p n t -> p (n t)").bitcast(I32))
 
         scale_win = keep.tile([P, T], U8, name="scale_win", tag="scales", align_bytes=64)
         nc.vector.memset(scale_win[:].bitcast(I32), 0)
@@ -51,14 +50,22 @@ def tile_picked_ydppg_rel_p_kernel(tc, x_words, x_scales, hT, proj, dres, qual, 
                 x_scales[0, 4 * quad : 4 * quad + 4, :].bitcast(I32),
             )
 
-        zeros = keep.tile([P, P], F32, name="zeros", tag="stage")
-        nc.vector.memset(zeros[:], 0.0)
+        ones = late.tile([P, P], F32, name="ones", offset=4 * T - 2 * P)
+        nc.vector.memset(ones[:], 1.0)
+        ramp = keep.tile([P, P], F32, name="ramp", align_bytes=64)
+        nc.vector.tensor_tensor_scan(ramp[:], ones[:], ones[:], 0.0, ALU.mult, ALU.add)
+        quad_first = keep.tile([P, 1], F32, name="quad_first")
+        for quad in range(4):
+            nc.vector.memset(quad_first[32 * quad : 32 * quad + 32, :], 32.0 * quad)
+        lane = keep.tile([P, 32], F32, name="lane", align_bytes=64)
+        nc.vector.transpose(lane[:], ramp[:, 0:32])
         ident = keep.tile([P, P], F32, name="ident")
-        nc.gpsimd.affine_select(
-            out=ident[:], in_=zeros[:], compare_op=ALU.not_equal, fill=1.0, base=0, pattern=[[-1, P]], channel_multiplier=1
-        )
+        nc.vector.tensor_scalar(ident[:], ramp[:], quad_first[:], lane[:, 0:1], ALU.subtract, ALU.is_equal)
 
-        stage = keep.tile([P, (3 * TILES - 1) * S + P], F32, name="stage", tag="stage")
+        word_win = late.tile([P, T], U32, name="word_win", offset=0)
+        nc.sync.dma_start(word_win[:].bitcast(I32), x_words[0].rearrange("p n t -> p (n t)").bitcast(I32))
+
+        stage = late.tile([P, (3 * TILES - 1) * S + P], F32, name="stage", offset=4 * T)
         proj_sb = [stage[:, i * S : (i + 1) * S] for i in range(TILES)]
         dres_sb = [stage[:, (TILES + i) * S : (TILES + i + 1) * S] for i in range(TILES)]
         h_second = stage[:, 2 * TILES * S : (2 * TILES + 1) * S].rearrange("p (j w) -> p j w", j=PACK)
@@ -72,9 +79,9 @@ def tile_picked_ydppg_rel_p_kernel(tc, x_words, x_scales, hT, proj, dres, qual, 
             nc.sync.dma_start(sb[i], src[i * P : (i + 1) * P, :])
 
         nc.sync.dma_start(h_second, h_rows[:, :, P : 2 * P])
+        nc.sync.dma_start(h_last, h_rows[:, :, 2 * P : V])
         load(proj_sb, proj, 0)
         load(proj_sb, proj, 1)
-        nc.sync.dma_start(h_last, h_rows[:, :, 2 * P : V])
         load(dres_sb, dres, 0)
         load(dres_sb, dres, 1)
         load(proj_sb, proj, 2)
@@ -105,7 +112,7 @@ def tile_picked_ydppg_rel_p_kernel(tc, x_words, x_scales, hT, proj, dres, qual, 
         grouped0 = cast(0)
         qual_win = keep.tile([P, T], F32, name="qual_win")
         for g in range(4):
-            spread = psum.tile([P, 4, P], F32, name="spread%d" % g, tag="turned", bufs=3)
+            spread = psum.tile([P, 4, P], F32, name="spread%d" % g, tag="bank%d" % g)
             for c in range(4):
                 col = 4 * g + c
                 nc.tensor.transpose(spread[:, c, :], q_rows[:, col : col + 1].to_broadcast([P, P]), ident[:])
@@ -122,7 +129,7 @@ def tile_picked_ydppg_rel_p_kernel(tc, x_words, x_scales, hT, proj, dres, qual, 
         q_sb = keep.tile([P, S], F32, name="q_sb")
         nc.vector.tensor_copy(q_sb[:], qual_win[:].indirect(offsets[:]))
 
-        inv_turned = psum.tile([P, P], F32, name="inv_turned", tag="turned", bufs=3)
+        inv_turned = psum.tile([P, P], F32, name="inv_turned", tag="bank3")
         nc.tensor.transpose(inv_turned[:], inv_rows, ident[:])
         inv_sb = keep.tile([P, TILES], F32, name="inv_sb")
         nc.scalar.copy(inv_sb[:], inv_turned[:, 0:TILES])
@@ -130,18 +137,23 @@ def tile_picked_ydppg_rel_p_kernel(tc, x_words, x_scales, hT, proj, dres, qual, 
         nc.scalar.activation(inv_fifth[:], inv_turned[:, 0:TILES], ACT.Copy, scale=0.2)
         quantise(1, cast(1))
 
-        q_col = None
+        q_turned = psum.tile([P, BLOCKS, P], F32, name="q_turned", tag="bank1")
+        for b in range(BLOCKS):
+            nc.tensor.transpose(q_turned[:, b, :], q_sb[:, b * P : (b + 1) * P], ident[:])
+        q_col = keep.tile([P, BLOCKS], F32, name="q_col")
+        nc.scalar.copy(q_col[:], q_turned[:, :, 0])
+
         minus, diff, square, fifth, rest, dnew, top, rtop, gain = {}, {}, {}, {}, {}, {}, {}, {}, {}
 
         def turned_proj(i):
-            turned = psum.tile([P, S], F32, name="turned%d" % i, tag="turned", bufs=3)
+            turned = psum.tile([P, S], F32, name="turned%d" % i, tag="bank%d" % i)
             for b in range(BLOCKS):
                 nc.tensor.transpose(turned[:, b * P : (b + 1) * P], proj_sb[i][:, b * P : (b + 1) * P], ident[:])
             minus[i] = keep.tile([P, S], F32, name="minus%d" % i)
             nc.scalar.activation(minus[i][:], turned[:], ACT.Copy, scale=-1.0)
 
         def product(i):
-            qy = psum.tile([P, S], F32, name="qy%d" % i, tag="qy", bufs=3)
+            qy = psum.tile([P, S], F32, name="qy%d" % i, tag="bank%d" % (4 + i % 3))
             if i in DIRECT_TILES:
                 nc.tensor.matmul_mx(
                     out=qy[:],
@@ -158,7 +170,7 @@ def tile_picked_ydppg_rel_p_kernel(tc, x_words, x_scales, hT, proj, dres, qual, 
             scaled = keep.tile([P, BLOCKS, P], F32, name="scaled%d" % i)
             width = BLOCKS
             for first in range(0, BLOCKS, width):
-                y_t = psum.tile([P, width, P], F32, name="y_t%d_%d" % (i, first), tag="y_t", bufs=2)
+                y_t = psum.tile([P, width, P], F32, name="y_t%d_%d" % (i, first), tag="bank%d" % (7 * (i % 2)))
                 for c in range(width):
                     b = first + c
                     nc.tensor.matmul_mx(
@@ -214,12 +226,12 @@ def tile_picked_ydppg_rel_p_kernel(tc, x_words, x_scales, hT, proj, dres, qual, 
             if i not in TURN_TILES:
                 nc.vector.scalar_tensor_tensor(gain[i][:, cols], dnew[i][:, cols], rtop[i][:], q_sb[:, cols], ALU.mult, ALU.mult)
                 return
-            dnew_t = psum.tile([P, BLOCKS, P], F32, name="dnew_t%d" % i, tag="turned", bufs=3)
+            dnew_t = psum.tile([P, BLOCKS, P], F32, name="dnew_t%d" % i, tag="bank%d" % (1 + i))
             for b in range(BLOCKS):
                 nc.tensor.transpose(dnew_t[:, b, :], dnew[i][:, b * P : (b + 1) * P], ident[:])
             for b in range(BLOCKS):
                 nc.scalar.activation(gain[i][:, b * P : (b + 1) * P], dnew_t[:, b, :], ACT.Copy, scale=q_col[:, b : b + 1])
-            back[i] = psum.tile([P, S], F32, name="back%d" % i, tag="qy", bufs=3)
+            back[i] = psum.tile([P, S], F32, name="back%d" % i, tag="bank%d" % (5 + i))
             for b in range(BLOCKS):
                 nc.tensor.transpose(back[i][:, b * P : (b + 1) * P], gain[i][:, b * P : (b + 1) * P], ident[:])
 
@@ -243,38 +255,38 @@ def tile_picked_ydppg_rel_p_kernel(tc, x_words, x_scales, hT, proj, dres, qual, 
         difference(0, qy0)
         squared(0)
         qy1 = product(1)
-        grouped2 = cast(2)
         difference(1, qy1)
         squared(1)
+        grouped2 = cast(2)
         quantise(2, grouped2)
         grouped3 = cast(3)
-        remainder(0)
         quantise(3, grouped3)
-        size(0)
-        best(0)
         qy2 = product(2)
-        invert(0)
+        remainder(0)
+        qy3 = product(3)
+        best(0)
         remainder(1)
-        weigh(0, whole)
+        invert(0)
         difference(2, qy2)
         squared(2)
-        finish(0, whole)
-        size(1)
+        weigh(0, whole)
+        size(0)
         best(1)
-        qy3 = product(3)
-        invert(1)
         difference(3, qy3)
         squared(3)
+        invert(1)
         weigh(1, whole)
+        size(1)
         remainder(2)
-        finish(1, whole)
-        size(2)
-        size(3)
+        finish(0, whole)
         best(2)
         remainder(3)
         invert(2)
-        best(3)
         weigh(2, whole)
+        size(2)
+        size(3)
+        best(3)
+        finish(1, whole)
         invert(3)
         finish(2, whole)
         weigh(3, left)

@@ -16,14 +16,15 @@ ALU = mybir.AluOpType
 ACT = mybir.ActivationFunctionType
 
 P = 128
+QUAD = 32
 PACK = 4
+LINE = 4
 TILES = V // P
 BLOCKS = S // P
-HALF = S // 2
+LAST = TILES - 1
+EARLY = 2
 FLOOR = 0.02
-PE_TILES = ()
-TURN_TILES = (0, 1, 2)
-DIRECT_TILES = (0, 1, 2)
+PENALTY = 0.2
 
 
 def tile_picked_ydppg_rel_p_kernel(tc, x_words, x_scales, hT, proj, dres, qual, inv, offs, out):
@@ -33,20 +34,26 @@ def tile_picked_ydppg_rel_p_kernel(tc, x_words, x_scales, hT, proj, dres, qual, 
         late = ctx.enter_context(tc.tile_pool(name="late", bufs=1))
         psum = ctx.enter_context(tc.psum_pool(name="psum", bufs=1))
 
+        def bank(number, shape, name):
+            return psum.tile(shape, F32, name=name, tag="bank%d" % number)
+
+        def block(b):
+            return slice(b * P, (b + 1) * P)
+
         offsets = keep.tile([P, S // 16], U16, name="offsets")
         nc.sync.dma_start(offsets[:], offs)
-
-        q_rows = keep.tile([P, T // P], F32, name="q_rows")
+        per_row = T // P
+        q_rows = keep.tile([P, per_row], F32, name="q_rows")
         nc.sync.dma_start(q_rows[:], qual[0:1, :].rearrange("o (p c) -> (o p) c", p=P))
         h_rows = hT.rearrange("(p j) w -> p j w", j=PACK)
-        h_first = keep.tile([P, PACK, P], F32, name="h_first")
-        nc.sync.dma_start(h_first[:], h_rows[:, :, 0:P])
+        h_early = keep.tile([P, PACK, EARLY * P], F32, name="h_early")
+        nc.sync.dma_start(h_early[:], h_rows[:, :, 0 : EARLY * P])
 
         scale_win = keep.tile([P, T], U8, name="scale_win", tag="scales", align_bytes=64)
         nc.vector.memset(scale_win[:].bitcast(I32), 0)
-        for quad in range(4):
+        for quad in range(P // QUAD):
             nc.scalar.dma_start(
-                scale_win[32 * quad : 32 * quad + 4, :].bitcast(I32),
+                scale_win[QUAD * quad : QUAD * quad + 4, :].bitcast(I32),
                 x_scales[0, 4 * quad : 4 * quad + 4, :].bitcast(I32),
             )
 
@@ -55,241 +62,205 @@ def tile_picked_ydppg_rel_p_kernel(tc, x_words, x_scales, hT, proj, dres, qual, 
         ramp = keep.tile([P, P], F32, name="ramp", align_bytes=64)
         nc.vector.tensor_tensor_scan(ramp[:], ones[:], ones[:], 0.0, ALU.mult, ALU.add)
         quad_first = keep.tile([P, 1], F32, name="quad_first")
-        for quad in range(4):
-            nc.vector.memset(quad_first[32 * quad : 32 * quad + 32, :], 32.0 * quad)
-        lane = keep.tile([P, 32], F32, name="lane", align_bytes=64)
-        nc.vector.transpose(lane[:], ramp[:, 0:32])
+        for quad in range(P // QUAD):
+            nc.vector.memset(quad_first[QUAD * quad : QUAD * (quad + 1), :], float(QUAD * quad))
+        lane = keep.tile([P, QUAD], F32, name="lane", align_bytes=64)
+        nc.vector.transpose(lane[:], ramp[:, 0:QUAD])
         ident = keep.tile([P, P], F32, name="ident")
         nc.vector.tensor_scalar(ident[:], ramp[:], quad_first[:], lane[:, 0:1], ALU.subtract, ALU.is_equal)
 
         word_win = late.tile([P, T], U32, name="word_win", offset=0)
         nc.sync.dma_start(word_win[:].bitcast(I32), x_words[0].rearrange("p n t -> p (n t)").bitcast(I32))
 
-        stage = late.tile([P, (3 * TILES - 1) * S + P], F32, name="stage", offset=4 * T)
+        h_late_first = 2 * TILES * S
+        inv_first = h_late_first + PACK * (TILES - EARLY) * P
+        stage = late.tile([P, inv_first + P], F32, name="stage", offset=4 * T)
         proj_sb = [stage[:, i * S : (i + 1) * S] for i in range(TILES)]
         dres_sb = [stage[:, (TILES + i) * S : (TILES + i + 1) * S] for i in range(TILES)]
-        h_second = stage[:, 2 * TILES * S : (2 * TILES + 1) * S].rearrange("p (j w) -> p j w", j=PACK)
-        h_last = stage[:, (2 * TILES + 1) * S : (3 * TILES - 1) * S].rearrange("p (j w) -> p j w", j=PACK)
-        h_raw = [h_first[:], h_second, h_last[:, :, 0:P], h_last[:, :, P : 2 * P]]
-        inv_rows = stage[:, (3 * TILES - 1) * S :]
+        h_late = stage[:, h_late_first:inv_first].rearrange("p (j w) -> p j w", j=PACK)
+        h_raw = [h_early[:, :, block(i)] for i in range(EARLY)] + [h_late[:, :, block(i)] for i in range(TILES - EARLY)]
+        inv_rows = stage[:, inv_first:]
         nc.vector.memset(inv_rows, 0.0)
         nc.sync.dma_start(inv_rows[0:TILES, :], inv.rearrange("(c p) o -> c (p o)", p=P))
+        nc.sync.dma_start(h_late, h_rows[:, :, EARLY * P : V])
+        for sb, src, tiles in ((proj_sb, proj, (0, 1)), (dres_sb, dres, (0,)), (proj_sb, proj, (2, 3)), (dres_sb, dres, (1, 2, 3))):
+            for i in tiles:
+                nc.sync.dma_start(sb[i], src[block(i), :])
 
-        def load(sb, src, i):
-            nc.sync.dma_start(sb[i], src[i * P : (i + 1) * P, :])
+        qual_win = keep.tile([P, T], F32, name="qual_win")
+        for g in range(per_row // LINE):
+            spread = bank(g, [P, LINE, P], "spread%d" % g)
+            for c in range(LINE):
+                col = LINE * g + c
+                nc.tensor.transpose(spread[:, c, :], q_rows[:, col : col + 1].to_broadcast([P, P]), ident[:])
+            nc.scalar.copy(
+                qual_win[:].rearrange("p (m c) -> p m c", c=per_row)[:, :, LINE * g : LINE * (g + 1)],
+                spread[:].rearrange("p c m -> p m c"),
+            )
 
-        nc.sync.dma_start(h_second, h_rows[:, :, P : 2 * P])
-        nc.sync.dma_start(h_last, h_rows[:, :, 2 * P : V])
-        load(proj_sb, proj, 0)
-        load(proj_sb, proj, 1)
-        load(dres_sb, dres, 0)
-        load(dres_sb, dres, 1)
-        load(proj_sb, proj, 2)
-        load(dres_sb, dres, 2)
-        load(proj_sb, proj, 3)
-        load(dres_sb, dres, 3)
-
-        h_codes, h_scales = [], []
+        h_codes, h_scales = {}, {}
 
         def cast(i):
             grouped = keep.tile([P, P, PACK], BF16, name="h_bf%d" % i, align_bytes=64)
-            nc.scalar.activation(
-                grouped[:].rearrange("p (c e) j -> p c j e", e=4),
-                h_raw[i].rearrange("p j (c e) -> p c j e", e=4),
-                ACT.Copy,
-            )
+            dst = grouped[:].rearrange("p (c e) j -> p c j e", e=LINE)
+            src = h_raw[i].rearrange("p j (c e) -> p c j e", e=LINE)
+            if i < EARLY:
+                nc.vector.tensor_copy(dst, src)
+            else:
+                nc.scalar.activation(dst, src, ACT.Copy)
             return grouped
 
         def quantise(i, grouped):
-            h_codes.append(keep.tile([P, P], U32, name="h_codes%d" % i, align_bytes=64))
-            h_scales.append(keep.tile([P, P], U8, name="h_scales%d" % i, align_bytes=64))
+            h_codes[i] = keep.tile([P, P], U32, name="h_codes%d" % i, align_bytes=64)
+            h_scales[i] = keep.tile([P, P], U8, name="h_scales%d" % i, align_bytes=64)
             nc.vector.quantize_mx(
                 out=h_codes[i][:].bitcast(FP8X4),
                 scales=h_scales[i][:],
                 in_=grouped[:].rearrange("p w j -> p (w j)"),
             )
 
-        grouped0 = cast(0)
-        qual_win = keep.tile([P, T], F32, name="qual_win")
-        for g in range(4):
-            spread = psum.tile([P, 4, P], F32, name="spread%d" % g, tag="bank%d" % g)
-            for c in range(4):
-                col = 4 * g + c
-                nc.tensor.transpose(spread[:, c, :], q_rows[:, col : col + 1].to_broadcast([P, P]), ident[:])
-            nc.scalar.copy(
-                qual_win[:].rearrange("p (m c) -> p m c", c=T // P)[:, :, 4 * g : 4 * g + 4],
-                spread[:].rearrange("p c m -> p m c"),
-            )
-
         x_bytes = keep.tile([P, S], U8, name="x_bytes", align_bytes=64)
         nc.vector.tensor_copy(x_bytes[:], scale_win[:].indirect(offsets[:]))
-        quantise(0, grouped0)
-        x_all = keep.tile([P, S], U32, name="x_all", tag="scales", align_bytes=64)
-        nc.vector.tensor_copy(x_all[:], word_win[:].indirect(offsets[:]))
-        q_sb = keep.tile([P, S], F32, name="q_sb")
-        nc.vector.tensor_copy(q_sb[:], qual_win[:].indirect(offsets[:]))
+        early_bf = [cast(i) for i in range(EARLY)]
+        for i in range(EARLY):
+            quantise(i, early_bf[i])
+        x_codes = keep.tile([P, S], U32, name="x_codes", tag="scales", align_bytes=64)
+        nc.vector.tensor_copy(x_codes[:], word_win[:].indirect(offsets[:]))
+        q_wide = keep.tile([P, S], F32, name="q_wide")
+        nc.vector.tensor_copy(q_wide[:], qual_win[:].indirect(offsets[:]))
 
-        inv_turned = psum.tile([P, P], F32, name="inv_turned", tag="bank3")
+        inv_turned = bank(3, [P, P], "inv_turned")
         nc.tensor.transpose(inv_turned[:], inv_rows, ident[:])
         inv_sb = keep.tile([P, TILES], F32, name="inv_sb")
         nc.scalar.copy(inv_sb[:], inv_turned[:, 0:TILES])
         inv_fifth = keep.tile([P, TILES], F32, name="inv_fifth")
-        nc.scalar.activation(inv_fifth[:], inv_turned[:, 0:TILES], ACT.Copy, scale=0.2)
-        quantise(1, cast(1))
+        nc.scalar.activation(inv_fifth[:], inv_turned[:, 0:TILES], ACT.Copy, scale=PENALTY)
 
-        q_turned = psum.tile([P, BLOCKS, P], F32, name="q_turned", tag="bank1")
-        for b in range(BLOCKS):
-            nc.tensor.transpose(q_turned[:, b, :], q_sb[:, b * P : (b + 1) * P], ident[:])
-        q_col = keep.tile([P, BLOCKS], F32, name="q_col")
-        nc.scalar.copy(q_col[:], q_turned[:, :, 0])
+        def new(name, i):
+            return keep.tile([P, S], F32, name="%s%d" % (name, i))
 
-        minus, diff, square, fifth, rest, dnew, top, rtop, gain = {}, {}, {}, {}, {}, {}, {}, {}, {}
+        def weighted_product(i):
+            y = bank(4 + i, [P, S], "y%d" % i)
+            nc.tensor.matmul_mx(
+                out=y[:],
+                lhsT=h_codes[i][:].bitcast(FP8X4),
+                lhsT_scale=h_scales[i][:],
+                rhs=x_codes[:].bitcast(FP8X4),
+                rhs_scale=x_bytes[:],
+                start=True,
+                stop=True,
+            )
+            weighted = new("weighted", i)
+            nc.vector.tensor_tensor(weighted[:], y[:], q_wide[:], ALU.mult)
+            return weighted
 
-        def turned_proj(i):
-            turned = psum.tile([P, S], F32, name="turned%d" % i, tag="bank%d" % i)
+        def difference_without_vector(i):
+            proj_t = bank(3, [P, S], "proj_t")
             for b in range(BLOCKS):
-                nc.tensor.transpose(turned[:, b * P : (b + 1) * P], proj_sb[i][:, b * P : (b + 1) * P], ident[:])
-            minus[i] = keep.tile([P, S], F32, name="minus%d" % i)
-            nc.scalar.activation(minus[i][:], turned[:], ACT.Copy, scale=-1.0)
-
-        def product(i):
-            qy = psum.tile([P, S], F32, name="qy%d" % i, tag="bank%d" % (4 + i % 3))
-            if i in DIRECT_TILES:
+                nc.tensor.transpose(proj_t[:, block(b)], proj_sb[i][:, block(b)], ident[:])
+            minus = new("minus", i)
+            nc.scalar.activation(minus[:], proj_t[:], ACT.Copy, scale=-1.0)
+            y_t = bank(7, [P, S], "y_t")
+            for b in range(BLOCKS):
                 nc.tensor.matmul_mx(
-                    out=qy[:],
-                    lhsT=h_codes[i][:].bitcast(FP8X4),
-                    lhsT_scale=h_scales[i][:],
-                    rhs=x_all[:].bitcast(FP8X4),
-                    rhs_scale=x_bytes[:],
+                    out=y_t[:, block(b)],
+                    lhsT=x_codes[:, block(b)].bitcast(FP8X4),
+                    lhsT_scale=x_bytes[:, block(b)],
+                    rhs=h_codes[i][:].bitcast(FP8X4),
+                    rhs_scale=h_scales[i][:],
                     start=True,
                     stop=True,
                 )
-                weighted = keep.tile([P, S], F32, name="weighted%d" % i)
-                nc.vector.tensor_tensor(weighted[:], qy[:], q_sb[:], ALU.mult)
-                return weighted
-            scaled = keep.tile([P, BLOCKS, P], F32, name="scaled%d" % i)
-            width = BLOCKS
-            for first in range(0, BLOCKS, width):
-                y_t = psum.tile([P, width, P], F32, name="y_t%d_%d" % (i, first), tag="bank%d" % (7 * (i % 2)))
-                for c in range(width):
-                    b = first + c
-                    nc.tensor.matmul_mx(
-                        out=y_t[:, c, :],
-                        lhsT=x_all[:, b * P : (b + 1) * P].bitcast(FP8X4),
-                        lhsT_scale=x_bytes[:, b * P : (b + 1) * P],
-                        rhs=h_codes[i][:].bitcast(FP8X4),
-                        rhs_scale=h_scales[i][:],
-                        start=True,
-                        stop=True,
-                    )
-                for c in range(width):
-                    b = first + c
-                    nc.scalar.activation(scaled[:, b, :], y_t[:, c, :], ACT.Copy, scale=q_col[:, b : b + 1])
+            scaled = new("scaled", i)
             for b in range(BLOCKS):
-                cols = slice(b * P, (b + 1) * P)
-                if i in PE_TILES:
-                    nc.tensor.matmul(qy[:, cols], minus[i][:, cols], ident[:], start=True, stop=False, is_transpose=True)
-                    nc.tensor.matmul(qy[:, cols], scaled[:, b, :], ident[:], start=False, stop=True, is_transpose=True)
-                else:
-                    nc.tensor.transpose(qy[:, cols], scaled[:, b, :], ident[:])
-            return qy
+                nc.scalar.activation(scaled[:, block(b)], y_t[:, block(b)], ACT.Copy, scale=q_col[:, b : b + 1])
+            total = bank(4, [P, S], "total")
+            for b in range(BLOCKS):
+                nc.tensor.matmul(total[:, block(b)], minus[:, block(b)], ident[:], start=True, stop=False, is_transpose=True)
+                nc.tensor.matmul(total[:, block(b)], scaled[:, block(b)], ident[:], start=False, stop=True, is_transpose=True)
+            return total
 
-        def difference(i, qy):
-            if i in PE_TILES:
-                diff[i] = qy
-            else:
-                diff[i] = keep.tile([P, S], F32, name="diff%d" % i)
-                nc.vector.tensor_tensor(diff[i][:], qy[:], proj_sb[i], ALU.subtract)
+        def gain_without_vector(i):
+            dnew_t = bank(1 + i, [P, S], "dnew_t%d" % i)
+            for b in range(BLOCKS):
+                nc.tensor.transpose(dnew_t[:, block(b)], dnew[i][:, block(b)], ident[:])
+            gain_t = new("gain_t", i)
+            for b in range(BLOCKS):
+                nc.scalar.activation(gain_t[:, block(b)], dnew_t[:, block(b)], ACT.Copy, scale=q_col[:, b : b + 1])
+            back = bank(5 + i, [P, S], "back%d" % i)
+            for b in range(BLOCKS):
+                nc.tensor.transpose(back[:, block(b)], gain_t[:, block(b)], ident[:])
+            return back
 
-        def squared(i):
-            square[i] = keep.tile([P, S], F32, name="square%d" % i)
+        late_bf = {i: cast(i) for i in range(EARLY, TILES)}
+        weighted = {i: weighted_product(i) for i in range(EARLY)}
+        q_turned = bank(1, [P, BLOCKS, P], "q_turned")
+        for b in range(BLOCKS):
+            nc.tensor.transpose(q_turned[:, b, :], q_wide[:, block(b)], ident[:])
+        q_col = keep.tile([P, BLOCKS], F32, name="q_col")
+        nc.scalar.copy(q_col[:], q_turned[:, :, 0])
+        for i in range(EARLY, TILES):
+            quantise(i, late_bf[i])
+
+        diff, square = {}, {}
+
+        def subtract_proj(i):
+            diff[i] = new("diff", i)
+            nc.vector.tensor_tensor(diff[i][:], weighted[i][:], proj_sb[i], ALU.subtract)
+
+        def square_of(i):
+            square[i] = new("square", i)
             nc.scalar.activation(square[i][:], diff[i][:], ACT.Square, scale=inv_sb[:, i : i + 1])
 
-        def size(i):
-            fifth[i] = keep.tile([P, S], F32, name="fifth%d" % i)
-            nc.scalar.activation(fifth[i][:], diff[i][:], ACT.Abs, scale=inv_fifth[:, i : i + 1])
+        for i in range(EARLY):
+            subtract_proj(i)
+            square_of(i)
+        for i in range(EARLY, LAST):
+            weighted[i] = weighted_product(i)
+        diff[LAST] = difference_without_vector(LAST)
+        for i in range(EARLY, LAST):
+            subtract_proj(i)
+            square_of(i)
+        square_of(LAST)
 
-        def remainder(i):
-            rest[i] = keep.tile([P, S], F32, name="rest%d" % i)
-            nc.vector.scalar_tensor_tensor(rest[i][:], dres_sb[i], FLOOR, square[i][:], ALU.add, ALU.subtract)
+        rest, dnew, top, rtop, gain = {}, {}, {}, {}, {}
 
-        def best(i):
-            dnew[i] = keep.tile([P, S], F32, name="dnew%d" % i)
-            top[i] = keep.tile([P, 1], F32, name="top%d" % i)
-            nc.vector.tensor_scalar(dnew[i][:], rest[i][:], FLOOR, None, ALU.max, ALU.max, accum_out=top[i][:])
-
-        def invert(i):
+        def invert_top(i):
             rtop[i] = keep.tile([P, 1], F32, name="rtop%d" % i)
             nc.vector.reciprocal(rtop[i][:], top[i][:])
 
-        def weigh(i, cols):
-            if i not in TURN_TILES:
-                nc.vector.scalar_tensor_tensor(gain[i][:, cols], dnew[i][:, cols], rtop[i][:], q_sb[:, cols], ALU.mult, ALU.mult)
-                return
-            dnew_t = psum.tile([P, BLOCKS, P], F32, name="dnew_t%d" % i, tag="bank%d" % (1 + i))
-            for b in range(BLOCKS):
-                nc.tensor.transpose(dnew_t[:, b, :], dnew[i][:, b * P : (b + 1) * P], ident[:])
-            for b in range(BLOCKS):
-                nc.scalar.activation(gain[i][:, b * P : (b + 1) * P], dnew_t[:, b, :], ACT.Copy, scale=q_col[:, b : b + 1])
-            back[i] = psum.tile([P, S], F32, name="back%d" % i, tag="bank%d" % (5 + i))
-            for b in range(BLOCKS):
-                nc.tensor.transpose(back[i][:, b * P : (b + 1) * P], gain[i][:, b * P : (b + 1) * P], ident[:])
+        for first in range(0, TILES, 2):
+            pair = (first, first + 1)
+            for i in pair:
+                rest[i] = new("rest", i)
+                nc.vector.scalar_tensor_tensor(rest[i][:], dres_sb[i], FLOOR, square[i][:], ALU.add, ALU.subtract)
+            for i in range(max(first - 2, 0), first):
+                invert_top(i)
+            for i in pair:
+                dnew[i] = new("dnew", i)
+                top[i] = keep.tile([P, 1], F32, name="top%d" % i)
+                nc.vector.tensor_scalar(dnew[i][:], rest[i][:], FLOOR, None, ALU.max, ALU.max, accum_out=top[i][:])
+            for i in pair:
+                if i < LAST:
+                    gain[i] = gain_without_vector(i)
 
-        def finish(i, cols):
-            if i in TURN_TILES:
-                nc.vector.scalar_tensor_tensor(
-                    result[i][:, cols], back[i][:, cols], rtop[i][:], fifth[i][:, cols], ALU.mult, ALU.subtract
-                )
-            else:
-                nc.vector.tensor_tensor(result[i][:, cols], gain[i][:, cols], fifth[i][:, cols], ALU.subtract)
-            nc.sync.dma_start(out[i * P : (i + 1) * P, cols], result[i][:, cols])
-
-        back = {}
-        result = {}
+        fifth = {}
         for i in range(TILES):
-            gain[i] = keep.tile([P, S], F32, name="gain%d" % i)
-            result[i] = keep.tile([P, S], F32, name="result%d" % i)
-        whole, left, right = slice(0, S), slice(0, HALF), slice(HALF, S)
-
-        qy0 = product(0)
-        difference(0, qy0)
-        squared(0)
-        qy1 = product(1)
-        difference(1, qy1)
-        squared(1)
-        grouped2 = cast(2)
-        quantise(2, grouped2)
-        grouped3 = cast(3)
-        quantise(3, grouped3)
-        qy2 = product(2)
-        remainder(0)
-        qy3 = product(3)
-        best(0)
-        remainder(1)
-        invert(0)
-        difference(2, qy2)
-        squared(2)
-        weigh(0, whole)
-        size(0)
-        best(1)
-        difference(3, qy3)
-        squared(3)
-        invert(1)
-        weigh(1, whole)
-        size(1)
-        remainder(2)
-        finish(0, whole)
-        best(2)
-        remainder(3)
-        invert(2)
-        weigh(2, whole)
-        size(2)
-        size(3)
-        best(3)
-        finish(1, whole)
-        invert(3)
-        finish(2, whole)
-        weigh(3, left)
-        weigh(3, right)
-        finish(3, left)
-        finish(3, right)
+            fifth[i] = new("fifth", i)
+            nc.scalar.activation(fifth[i][:], diff[i][:], ACT.Abs, scale=inv_fifth[:, i : i + 1])
+        for i in range(TILES - 2, TILES):
+            invert_top(i)
+        for i in range(LAST):
+            result = new("result", i)
+            nc.vector.scalar_tensor_tensor(result[:], gain[i][:], rtop[i][:], fifth[i][:], ALU.mult, ALU.subtract)
+            nc.sync.dma_start(out[block(i), :], result[:])
+        halves = (slice(0, S // 2), slice(S // 2, S))
+        gain[LAST] = new("gain", LAST)
+        result = new("result", LAST)
+        for cols in halves:
+            nc.vector.scalar_tensor_tensor(
+                gain[LAST][:, cols], dnew[LAST][:, cols], rtop[LAST][:], q_wide[:, cols], ALU.mult, ALU.mult
+            )
+        for cols in halves:
+            nc.vector.tensor_tensor(result[:, cols], gain[LAST][:, cols], fifth[LAST][:, cols], ALU.subtract)
+            nc.sync.dma_start(out[block(LAST), cols], result[:, cols])

from contextlib import ExitStack

import concourse.mybir as mybir

K, T, S, V = 512, 2048, 512, 512
FLOPS = 2 * K * S * V

F32 = mybir.dt.float32
BF16 = mybir.dt.bfloat16
I32 = mybir.dt.int32
U32 = mybir.dt.uint32
U16 = mybir.dt.uint16
U8 = mybir.dt.uint8
FP8X4 = mybir.dt.float8_e4m3fn_x4
ALU = mybir.AluOpType
ACT = mybir.ActivationFunctionType

P = 128
QUAD = 32
PACK = 4
LINE = 4
TILES = V // P
BLOCKS = S // P
LAST = TILES - 1
EARLY = 2
FLOOR = 0.02
PENALTY = 0.2


def tile_picked_ydppg_rel_p_kernel(tc, x_words, x_scales, hT, proj, dres, qual, inv, offs, out):
    nc = tc.nc
    with ExitStack() as ctx:
        keep = ctx.enter_context(tc.tile_pool(name="keep", bufs=1))
        late = ctx.enter_context(tc.tile_pool(name="late", bufs=1))
        psum = ctx.enter_context(tc.psum_pool(name="psum", bufs=1))

        def bank(number, shape, name):
            return psum.tile(shape, F32, name=name, tag="bank%d" % number)

        def block(b):
            return slice(b * P, (b + 1) * P)

        offsets = keep.tile([P, S // 16], U16, name="offsets")
        nc.sync.dma_start(offsets[:], offs)
        per_row = T // P
        q_rows = keep.tile([P, per_row], F32, name="q_rows")
        nc.sync.dma_start(q_rows[:], qual[0:1, :].rearrange("o (p c) -> (o p) c", p=P))
        h_rows = hT.rearrange("(p j) w -> p j w", j=PACK)
        h_early = keep.tile([P, PACK, EARLY * P], F32, name="h_early")
        nc.sync.dma_start(h_early[:], h_rows[:, :, 0 : EARLY * P])

        scale_win = keep.tile([P, T], U8, name="scale_win", tag="scales", align_bytes=64)
        nc.vector.memset(scale_win[:].bitcast(I32), 0)
        for quad in range(P // QUAD):
            nc.scalar.dma_start(
                scale_win[QUAD * quad : QUAD * quad + 4, :].bitcast(I32),
                x_scales[0, 4 * quad : 4 * quad + 4, :].bitcast(I32),
            )

        ones = late.tile([P, P], F32, name="ones", offset=4 * T - 2 * P)
        nc.vector.memset(ones[:], 1.0)
        ramp = keep.tile([P, P], F32, name="ramp", align_bytes=64)
        nc.vector.tensor_tensor_scan(ramp[:], ones[:], ones[:], 0.0, ALU.mult, ALU.add)
        quad_first = keep.tile([P, 1], F32, name="quad_first")
        for quad in range(P // QUAD):
            nc.vector.memset(quad_first[QUAD * quad : QUAD * (quad + 1), :], float(QUAD * quad))
        lane = keep.tile([P, QUAD], F32, name="lane", align_bytes=64)
        nc.vector.transpose(lane[:], ramp[:, 0:QUAD])
        ident = keep.tile([P, P], F32, name="ident")
        nc.vector.tensor_scalar(ident[:], ramp[:], quad_first[:], lane[:, 0:1], ALU.subtract, ALU.is_equal)

        word_win = late.tile([P, T], U32, name="word_win", offset=0)
        nc.sync.dma_start(word_win[:].bitcast(I32), x_words[0].rearrange("p n t -> p (n t)").bitcast(I32))

        h_late_first = 2 * TILES * S
        inv_first = h_late_first + PACK * (TILES - EARLY) * P
        stage = late.tile([P, inv_first + P], F32, name="stage", offset=4 * T)
        proj_sb = [stage[:, i * S : (i + 1) * S] for i in range(TILES)]
        dres_sb = [stage[:, (TILES + i) * S : (TILES + i + 1) * S] for i in range(TILES)]
        h_late = stage[:, h_late_first:inv_first].rearrange("p (j w) -> p j w", j=PACK)
        h_raw = [h_early[:, :, block(i)] for i in range(EARLY)] + [h_late[:, :, block(i)] for i in range(TILES - EARLY)]
        inv_rows = stage[:, inv_first:]
        nc.vector.memset(inv_rows, 0.0)
        nc.sync.dma_start(inv_rows[0:TILES, :], inv.rearrange("(c p) o -> c (p o)", p=P))
        nc.sync.dma_start(h_late, h_rows[:, :, EARLY * P : V])
        for sb, src, tiles in ((proj_sb, proj, (0, 1)), (dres_sb, dres, (0,)), (proj_sb, proj, (2, 3)), (dres_sb, dres, (1, 2, 3))):
            for i in tiles:
                nc.sync.dma_start(sb[i], src[block(i), :])

        qual_win = keep.tile([P, T], F32, name="qual_win")
        for g in range(per_row // LINE):
            spread = bank(g, [P, LINE, P], "spread%d" % g)
            for c in range(LINE):
                col = LINE * g + c
                nc.tensor.transpose(spread[:, c, :], q_rows[:, col : col + 1].to_broadcast([P, P]), ident[:])
            nc.scalar.copy(
                qual_win[:].rearrange("p (m c) -> p m c", c=per_row)[:, :, LINE * g : LINE * (g + 1)],
                spread[:].rearrange("p c m -> p m c"),
            )

        h_codes, h_scales = {}, {}

        def cast(i):
            grouped = keep.tile([P, P, PACK], BF16, name="h_bf%d" % i, align_bytes=64)
            dst = grouped[:].rearrange("p (c e) j -> p c j e", e=LINE)
            src = h_raw[i].rearrange("p j (c e) -> p c j e", e=LINE)
            if i < EARLY:
                nc.vector.tensor_copy(dst, src)
            else:
                nc.scalar.activation(dst, src, ACT.Copy)
            return grouped

        def quantise(i, grouped):
            h_codes[i] = keep.tile([P, P], U32, name="h_codes%d" % i, align_bytes=64)
            h_scales[i] = keep.tile([P, P], U8, name="h_scales%d" % i, align_bytes=64)
            nc.vector.quantize_mx(
                out=h_codes[i][:].bitcast(FP8X4),
                scales=h_scales[i][:],
                in_=grouped[:].rearrange("p w j -> p (w j)"),
            )

        x_bytes = keep.tile([P, S], U8, name="x_bytes", align_bytes=64)
        nc.vector.tensor_copy(x_bytes[:], scale_win[:].indirect(offsets[:]))
        early_bf = [cast(i) for i in range(EARLY)]
        for i in range(EARLY):
            quantise(i, early_bf[i])
        x_codes = keep.tile([P, S], U32, name="x_codes", tag="scales", align_bytes=64)
        nc.vector.tensor_copy(x_codes[:], word_win[:].indirect(offsets[:]))
        q_wide = keep.tile([P, S], F32, name="q_wide")
        nc.vector.tensor_copy(q_wide[:], qual_win[:].indirect(offsets[:]))

        inv_turned = bank(3, [P, P], "inv_turned")
        nc.tensor.transpose(inv_turned[:], inv_rows, ident[:])
        inv_sb = keep.tile([P, TILES], F32, name="inv_sb")
        nc.scalar.copy(inv_sb[:], inv_turned[:, 0:TILES])
        inv_fifth = keep.tile([P, TILES], F32, name="inv_fifth")
        nc.scalar.activation(inv_fifth[:], inv_turned[:, 0:TILES], ACT.Copy, scale=PENALTY)

        def new(name, i):
            return keep.tile([P, S], F32, name="%s%d" % (name, i))

        def weighted_product(i):
            y = bank(4 + i, [P, S], "y%d" % i)
            nc.tensor.matmul_mx(
                out=y[:],
                lhsT=h_codes[i][:].bitcast(FP8X4),
                lhsT_scale=h_scales[i][:],
                rhs=x_codes[:].bitcast(FP8X4),
                rhs_scale=x_bytes[:],
                start=True,
                stop=True,
            )
            weighted = new("weighted", i)
            nc.vector.tensor_tensor(weighted[:], y[:], q_wide[:], ALU.mult)
            return weighted

        def difference_without_vector(i):
            proj_t = bank(3, [P, S], "proj_t")
            for b in range(BLOCKS):
                nc.tensor.transpose(proj_t[:, block(b)], proj_sb[i][:, block(b)], ident[:])
            minus = new("minus", i)
            nc.scalar.activation(minus[:], proj_t[:], ACT.Copy, scale=-1.0)
            y_t = bank(7, [P, S], "y_t")
            for b in range(BLOCKS):
                nc.tensor.matmul_mx(
                    out=y_t[:, block(b)],
                    lhsT=x_codes[:, block(b)].bitcast(FP8X4),
                    lhsT_scale=x_bytes[:, block(b)],
                    rhs=h_codes[i][:].bitcast(FP8X4),
                    rhs_scale=h_scales[i][:],
                    start=True,
                    stop=True,
                )
            scaled = new("scaled", i)
            for b in range(BLOCKS):
                nc.scalar.activation(scaled[:, block(b)], y_t[:, block(b)], ACT.Copy, scale=q_col[:, b : b + 1])
            total = bank(4, [P, S], "total")
            for b in range(BLOCKS):
                nc.tensor.matmul(total[:, block(b)], minus[:, block(b)], ident[:], start=True, stop=False, is_transpose=True)
                nc.tensor.matmul(total[:, block(b)], scaled[:, block(b)], ident[:], start=False, stop=True, is_transpose=True)
            return total

        def gain_without_vector(i):
            dnew_t = bank(1 + i, [P, S], "dnew_t%d" % i)
            for b in range(BLOCKS):
                nc.tensor.transpose(dnew_t[:, block(b)], dnew[i][:, block(b)], ident[:])
            gain_t = new("gain_t", i)
            for b in range(BLOCKS):
                nc.scalar.activation(gain_t[:, block(b)], dnew_t[:, block(b)], ACT.Copy, scale=q_col[:, b : b + 1])
            back = bank(5 + i, [P, S], "back%d" % i)
            for b in range(BLOCKS):
                nc.tensor.transpose(back[:, block(b)], gain_t[:, block(b)], ident[:])
            return back

        late_bf = {i: cast(i) for i in range(EARLY, TILES)}
        weighted = {i: weighted_product(i) for i in range(EARLY)}
        q_turned = bank(1, [P, BLOCKS, P], "q_turned")
        for b in range(BLOCKS):
            nc.tensor.transpose(q_turned[:, b, :], q_wide[:, block(b)], ident[:])
        q_col = keep.tile([P, BLOCKS], F32, name="q_col")
        nc.scalar.copy(q_col[:], q_turned[:, :, 0])
        for i in range(EARLY, TILES):
            quantise(i, late_bf[i])

        diff, square = {}, {}

        def subtract_proj(i):
            diff[i] = new("diff", i)
            nc.vector.tensor_tensor(diff[i][:], weighted[i][:], proj_sb[i], ALU.subtract)

        def square_of(i):
            square[i] = new("square", i)
            nc.scalar.activation(square[i][:], diff[i][:], ACT.Square, scale=inv_sb[:, i : i + 1])

        for i in range(EARLY):
            subtract_proj(i)
            square_of(i)
        for i in range(EARLY, LAST):
            weighted[i] = weighted_product(i)
        diff[LAST] = difference_without_vector(LAST)
        for i in range(EARLY, LAST):
            subtract_proj(i)
            square_of(i)
        square_of(LAST)

        rest, dnew, top, rtop, gain = {}, {}, {}, {}, {}

        def invert_top(i):
            rtop[i] = keep.tile([P, 1], F32, name="rtop%d" % i)
            nc.vector.reciprocal(rtop[i][:], top[i][:])

        for first in range(0, TILES, 2):
            pair = (first, first + 1)
            for i in pair:
                rest[i] = new("rest", i)
                nc.vector.scalar_tensor_tensor(rest[i][:], dres_sb[i], FLOOR, square[i][:], ALU.add, ALU.subtract)
            for i in range(max(first - 2, 0), first):
                invert_top(i)
            for i in pair:
                dnew[i] = new("dnew", i)
                top[i] = keep.tile([P, 1], F32, name="top%d" % i)
                nc.vector.tensor_scalar(dnew[i][:], rest[i][:], FLOOR, None, ALU.max, ALU.max, accum_out=top[i][:])
            for i in pair:
                if i < LAST:
                    gain[i] = gain_without_vector(i)

        fifth = {}
        for i in range(TILES):
            fifth[i] = new("fifth", i)
            nc.scalar.activation(fifth[i][:], diff[i][:], ACT.Abs, scale=inv_fifth[:, i : i + 1])
        for i in range(TILES - 2, TILES):
            invert_top(i)
        for i in range(LAST):
            result = new("result", i)
            nc.vector.scalar_tensor_tensor(result[:], gain[i][:], rtop[i][:], fifth[i][:], ALU.mult, ALU.subtract)
            nc.sync.dma_start(out[block(i), :], result[:])
        halves = (slice(0, S // 2), slice(S // 2, S))
        gain[LAST] = new("gain", LAST)
        result = new("result", LAST)
        for cols in halves:
            nc.vector.scalar_tensor_tensor(
                gain[LAST][:, cols], dnew[LAST][:, cols], rtop[LAST][:], q_wide[:, cols], ALU.mult, ALU.mult
            )
        for cols in halves:
            nc.vector.tensor_tensor(result[:, cols], gain[LAST][:, cols], fifth[LAST][:, cols], ALU.subtract)
            nc.sync.dma_start(out[block(LAST), cols], result[:, cols])
